import numpy as np
import ml_dtypes


def mxq(x, axis, fmt="e4m3"):
    dtype, down = {"e4m3": (ml_dtypes.float8_e4m3fn, 7), "e5m2": (ml_dtypes.float8_e5m2, 14)}[fmt]
    v = np.moveaxis(np.asarray(x, np.float32).astype(ml_dtypes.bfloat16).astype(np.float64), axis, -1)
    blocks = v.reshape(v.shape[:-1] + (-1, 32))
    amax = np.abs(blocks).max(-1, keepdims=True)
    byte = np.maximum(np.where(amax > 0, np.frexp(amax)[1] - 1 + 127, 0) - down, 1)
    scale = np.exp2(byte - 127.0)
    codes = (blocks / scale).astype(np.float32).astype(dtype).astype(np.float64)
    return np.moveaxis((codes * scale).reshape(v.shape), -1, axis)


WIDE = False


def mx_kscale(k):
    if not WIDE:
        return np.ones(k)
    levels = np.array([30, -30])
    if k % 512:
        return np.exp2(np.random.permutation(np.resize(levels, k // 32))).repeat(32)
    a = np.empty((k // 512, 16))
    for p in range(k // 512):
        a[p, :8] = np.random.permutation(np.resize(levels, 8))
        for g in range(8):
            far = levels[np.abs(levels - a[p, g]) >= 10]
            a[p, g + 8] = far[np.random.randint(len(far))]
    return np.exp2(a.ravel()).repeat(32)


def f64(x):
    return np.asarray(x).astype(np.float64)


def striped(idx):
    return np.tile(np.asarray(idx).reshape(-1, 16).T, (8, 1)).astype(np.uint16)


def unstriped(offs):
    return offs[:16].T.reshape(-1).astype(np.int64)


def striped8(idx):
    return np.asarray(idx).reshape(8, -1, 16).transpose(0, 2, 1).reshape(128, -1).astype(np.uint16)


def unstriped8(offs):
    return offs.reshape(8, 16, -1).transpose(0, 2, 1).reshape(8, -1).astype(np.int64)


def pick8(x, idx, run):
    r = np.arange(len(x))
    return x[r[:, None], idx[r % (8 * run) // run]]


E2M1 = np.array([0.0, 0.5, 1.0, 1.5, 2.0, 3.0, 4.0, 6.0, -0.0, -0.5, -1.0, -1.5, -2.0, -3.0, -4.0, -6.0])


def pack_weight(w, fmt):
    k, n = w.shape
    w = f64(np.asarray(w, np.float32).astype(ml_dtypes.bfloat16)).reshape(k // 32, 32, n)
    amax = np.abs(w).max(1)
    if fmt in ("e4m3", "e5m2"):
        byte = np.frexp(amax)[1] - 1 + 127 - (7 if fmt == "e4m3" else 14)
    else:
        mant, ex = np.frexp(amax / 6.0)
        byte = np.where(mant > 0.5, ex, ex - 1) + 127
    byte = np.clip(np.where(amax > 0, byte, 1), 1, 254)
    scaled = (w * np.exp2(127.0 - byte)[:, None, :]).reshape(k, n).astype(np.float32)
    by_word = np.ascontiguousarray(scaled.reshape(k // 512, 128, 4, n).transpose(0, 1, 3, 2))
    if fmt in ("e4m3", "e5m2"):
        words = by_word.astype(ml_dtypes.float8_e4m3fn if fmt == "e4m3" else ml_dtypes.float8_e5m2).view(np.uint8)
    else:
        c = by_word.astype(ml_dtypes.float4_e2m1fn).view(np.uint8) & 0xF
        words = (c[..., 0::2] | (c[..., 1::2] << 4)).reshape(k // 512, 128, 2 * n)
    return np.ascontiguousarray(words), np.ascontiguousarray(byte.astype(np.uint8).reshape(k // 512, 16, n))


def unpack_weight(words, scales, fmt):
    g, _, n = scales.shape
    words = np.ascontiguousarray(words).reshape(g, 128, n, -1)
    if fmt in ("e4m3", "e5m2"):
        vals = words.view(ml_dtypes.float8_e4m3fn if fmt == "e4m3" else ml_dtypes.float8_e5m2).astype(np.float64)
    else:
        nib = np.empty((g, 128, n, 4), np.uint8)
        nib[..., 0::2] = words & 0xF
        nib[..., 1::2] = words >> 4
        vals = E2M1[nib]
    vals = vals * np.repeat(np.exp2(scales.astype(np.float64) - 127.0), 8, axis=1)[..., None]
    return vals.transpose(0, 1, 3, 2).reshape(g * 512, n)


K, T, J, R, C, O, N, E = 512, 2048, 256, 512, 512, 128, 256, 512


def setup_inputs():
    n = np.random.standard_normal
    idx = np.random.permutation(T)[:J]
    idx2 = np.random.permutation(T)[:J]
    idx3 = np.stack([np.random.permutation(C)[:J] for _ in range(8)])
    idx4 = np.stack([np.random.permutation(C)[:O] for _ in range(8)])
    idx5 = np.random.permutation(J)[:O]
    idx6 = np.random.permutation(E)[:O]
    idx7 = np.random.permutation(E)[:O]
    fk = mx_kscale(K)
    fr = mx_kscale(R)
    xtp = pack_weight(n((K, T)) / fk[:, None], "e5m2")
    wp = pack_weight(n((K, R)) * 1 / np.sqrt(K) * fk[:, None] * fr, "e2m1")
    w2p = pack_weight(n((K, R)) * 1 / np.sqrt(K) * fk[:, None], "e4m3")
    wbp = pack_weight(n((R, N)) * 1 / np.sqrt(R) / fr[:, None], "e2m1")
    return {
        "xt_words": xtp[0],
        "xt_scales": xtp[1],
        "w_words": wp[0],
        "w_scales": wp[1],
        "w2_words": w2p[0],
        "w2_scales": w2p[1],
        "wb_words": wbp[0],
        "wb_scales": wbp[1],
        "offs": striped(idx),
        "offs2": striped(idx2),
        "offs3": striped8(idx3),
        "offs4": striped8(idx4),
        "offs5": striped(idx5),
        "offs6": striped(idx6),
        "offs7": striped(idx7),
    }


def reference(xt_words, xt_scales, w_words, w_scales, w2_words, w2_scales, wb_words, wb_scales, offs, offs2, offs3, offs4, offs5, offs6, offs7):
    idx = unstriped(offs)
    idx2 = unstriped(offs2)
    idx3 = unstriped8(offs3)
    idx4 = unstriped8(offs4)
    idx5 = unstriped(offs5)
    idx6 = unstriped(offs6)
    idx7 = unstriped(offs7)
    xtu = unpack_weight(xt_words, xt_scales, "e5m2")
    wu = unpack_weight(w_words, w_scales, "e2m1")
    w2u = unpack_weight(w2_words, w2_scales, "e4m3")
    wbu = unpack_weight(wb_words, wb_scales, "e2m1")
    xtidxg = xtu[:, idx]
    a = wu.T @ xtidxg
    xtidx2g = xtu[:, idx2]
    b = w2u.T @ xtidx2g
    lb = b[:, 0:1]
    la = a[:, 0:1]
    pw = np.zeros((R, C))
    pw[np.arange(R)[:, None], idx3[np.arange(R) % 512 // 64]] = a
    hid = np.abs(pick8(pw, idx4, 64) * lb - b[:, idx5] * la)
    hidq = mxq(hid, 0, "e4m3")
    p = wbu.T @ hidq
    pa = np.zeros((N, E))
    pa[:, idx6] = p
    pb = np.zeros((N, E))
    pb[:, idx7] = p
    y = pa + pb
    return y

@@ -1,0 +1,216 @@
+from contextlib import ExitStack
+
+import concourse.mybir as mybir
+
+K, T, J, R, C, O, N, E = 512, 2048, 256, 512, 512, 128, 256, 512
+FLOPS = 2 * K * R * J * 2 + 2 * R * N * O
+
+F32 = mybir.dt.float32
+BF16 = mybir.dt.bfloat16
+I32 = mybir.dt.int32
+U32 = mybir.dt.uint32
+U16 = mybir.dt.uint16
+U8 = mybir.dt.uint8
+E4M3 = mybir.dt.float8_e4m3fn_x4
+E5M2 = mybir.dt.float8_e5m2_x4
+E2M1 = mybir.dt.float4_e2m1fn_x4
+ACT = mybir.ActivationFunctionType
+ALU = mybir.AluOpType
+
+P = 128
+PACK = 4
+QUADS = 4
+
+
+def tile_list_leadgroupboard_ahead_one_pagetwice_kernel(
+    tc, xt_words, xt_scales, w_words, w_scales, w2_words, w2_scales, wb_words, wb_scales,
+    offs, offs2, offs3, offs4, offs5, offs6, offs7, out,
+):
+    nc = tc.nc
+    with ExitStack() as ctx:
+        lists = ctx.enter_context(tc.tile_pool(name="lists", bufs=1))
+        keep = ctx.enter_context(tc.tile_pool(name="keep", bufs=1))
+        psum = ctx.enter_context(tc.psum_pool(name="psum", bufs=1))
+
+        def load_list(name, src):
+            tile = lists.tile(list(src.shape), U16, name=name)
+            nc.sync.dma_start(tile[:], src)
+            return tile
+
+        def zeroed_plane(name, width):
+            plane = keep.tile([P, width], U8, name=name, align_bytes=64)
+            nc.vector.memset(plane[:].bitcast(I32), 0)
+            return plane
+
+        def load_plane(queue, plane, scales):
+            for q in range(QUADS):
+                queue.dma_start(
+                    out=plane[32 * q : 32 * q + 4, :].bitcast(I32),
+                    in_=scales[0, 4 * q : 4 * q + 4, :].bitcast(I32),
+                )
+
+        def load_stage(queue, name, scales):
+            stage = keep.tile([4, QUADS, R // 4], I32, name=name)
+            queue.dma_start(out=stage[:], in_=scales[0].bitcast(I32).rearrange("(q r) c -> r q c", r=4))
+            return stage
+
+        def dealt_plane(name, stage, plane):
+            for q in range(QUADS):
+                nc.vector.tensor_copy(out=plane[32 * q : 32 * q + 4, :].bitcast(I32), in_=stage[:, q, :])
+            dealt = keep.tile([P, R], U8, name=name, align_bytes=64)
+            nc.vector.tensor_copy(
+                out=dealt[:].rearrange("p (t m) -> p t m", t=PACK),
+                in_=plane[:].rearrange("p (m t) -> p t m", t=PACK),
+            )
+            return dealt
+
+        xs = zeroed_plane("xs", T)
+        o1 = load_list("o1", offs)
+        ws_stage = load_stage(nc.scalar, "ws_stage", w_scales)
+        o2 = load_list("o2", offs2)
+        xw = keep.tile([P, T], I32, name="xw", align_bytes=64)
+        nc.sync.dma_start(out=xw[:], in_=xt_words[0].rearrange("p c t -> p (c t)").bitcast(I32))
+        load_plane(nc.scalar, xs, xt_scales)
+        w2s_stage = load_stage(nc.scalar, "w2s_stage", w2_scales)
+        ww = keep.tile([P, R // 2], I32, name="ww", align_bytes=64)
+        nc.sync.dma_start(out=ww[:], in_=w_words[0].bitcast(I32))
+        w2w = keep.tile([P, R], I32, name="w2w", align_bytes=64)
+        nc.sync.dma_start(out=w2w[:], in_=w2_words[0].rearrange("p c t -> p (c t)").bitcast(I32))
+        o3 = load_list("o3", offs3)
+        o5 = load_list("o5", offs5)
+        o4 = load_list("o4", offs4)
+        wbw = keep.tile([P, 2 * N], U8, name="wbw", align_bytes=64)
+        nc.sync.dma_start(out=wbw[:].bitcast(I32), in_=wb_words[0].bitcast(I32))
+        ws = zeroed_plane("ws", R)
+        w2s = zeroed_plane("w2s", R)
+        wbs = zeroed_plane("wbs", N)
+        load_plane(nc.sync, wbs, wb_scales)
+        o6 = load_list("o6", offs6)
+        o7 = load_list("o7", offs7)
+
+        boards = []
+        for t in range(PACK):
+            board = keep.tile([P, C], F32, name="board%d" % t)
+            nc.vector.memset(board[:], 0.0)
+            boards.append(board)
+
+        ws_dealt = dealt_plane("ws_dealt", ws_stage, ws)
+
+        def gather_scales(name, offsets):
+            picked = keep.tile([P, J], U8, name=name, align_bytes=64)
+            nc.vector.tensor_copy(out=picked[:], in_=xs[:].indirect(offsets[:]))
+            return picked
+
+        def gather_words(name, offsets):
+            picked = keep.tile([P, J], I32, name=name, align_bytes=64)
+            nc.vector.tensor_copy(out=picked[:].bitcast(U32), in_=xw[:].bitcast(U32).indirect(offsets[:]))
+            return picked
+
+        xs1 = gather_scales("xs1", o1)
+        xs2 = gather_scales("xs2", o2)
+        w2s_dealt = dealt_plane("w2s_dealt", w2s_stage, w2s)
+        xw1 = gather_words("xw1", o1)
+        xw2 = gather_words("xw2", o2)
+
+        ww_dealt = keep.tile([P, 2 * R], U8, name="ww_dealt", align_bytes=64)
+        ww_out = ww_dealt[:].bitcast(U16).rearrange("p (t m) -> p t m", t=PACK)
+        ww_in = ww[:].bitcast(U16).rearrange("p (m t) -> p t m", t=PACK)
+        nc.scalar.copy(out=ww_out[:, 0, :], in_=ww_in[:, 0, :])
+        nc.scalar.copy(out=ww_out[:, 1:, :], in_=ww_in[:, 1:, :])
+
+        a_rows = []
+        for t in range(PACK):
+            acc = psum.tile([P, J], F32, name="acc_a%d" % t, tag="bank%d" % t)
+            nc.tensor.matmul_mx(
+                out=acc[:],
+                lhsT=ww_dealt[:, 2 * P * t : 2 * P * (t + 1)].bitcast(E2M1),
+                lhsT_scale=ws_dealt[:, P * t : P * (t + 1)],
+                rhs=xw1[:].bitcast(E5M2),
+                rhs_scale=xs1[:],
+                start=True,
+                stop=True,
+            )
+            a_t = keep.tile([P, J], F32, name="a%d" % t)
+            nc.scalar.copy(out=a_t[:], in_=acc[:])
+            nc.vector.tensor_copy(out=boards[t][:].indirect(o3[:]), in_=a_t[:])
+            a_rows.append(a_t)
+
+        w2w_dealt = keep.tile([P, R], I32, name="w2w_dealt", align_bytes=64)
+        nc.scalar.copy(
+            out=w2w_dealt[:].bitcast(U32).rearrange("p (t m) -> p t m", t=PACK),
+            in_=w2w[:].bitcast(U32).rearrange("p (m t) -> p t m", t=PACK),
+        )
+
+        from_board = keep.tile([P, PACK, O], F32, name="from_board", tag="reuse0", align_bytes=64)
+        from_b = keep.tile([P, PACK, O], F32, name="from_b", tag="reuse1", align_bytes=64)
+        b_rows = []
+        for t in range(PACK):
+            acc = psum.tile([P, J], F32, name="acc_b%d" % t, tag="bank%d" % (PACK + t))
+            nc.tensor.matmul_mx(
+                out=acc[:],
+                lhsT=w2w_dealt[:, P * t : P * (t + 1)].bitcast(E4M3),
+                lhsT_scale=w2s_dealt[:, P * t : P * (t + 1)],
+                rhs=xw2[:].bitcast(E5M2),
+                rhs_scale=xs2[:],
+                start=True,
+                stop=True,
+            )
+            b_t = keep.tile([P, J], F32, name="b%d" % t)
+            nc.scalar.copy(out=b_t[:], in_=acc[:])
+            nc.scalar.activation(
+                out=from_b[:, t, :], in_=b_t[:].indirect(o5[:]), func=ACT.Copy, scale=a_rows[t][:, 0:1]
+            )
+            b_rows.append(b_t)
+        for t in range(PACK):
+            nc.scalar.activation(
+                out=from_board[:, t, :], in_=boards[t][:].indirect(o4[:]), func=ACT.Copy, scale=b_rows[t][:, 0:1]
+            )
+
+        diff = keep.tile([P, PACK, O], F32, name="diff", tag="reuse2", align_bytes=64)
+        hid = keep.tile([P, O, PACK], BF16, name="hid", tag="reuse3", align_bytes=64)
+        for t0 in (0, 2):
+            pair = slice(t0, t0 + 2)
+            nc.vector.tensor_tensor(
+                out=diff[:, pair, :], in0=from_board[:, pair, :], in1=from_b[:, pair, :], op=ALU.subtract
+            )
+            nc.scalar.activation(
+                out=hid[:, :, pair], in_=diff[:, pair, :].rearrange("p t o -> p o t"), func=ACT.Abs
+            )
+        hid_words = keep.tile([P, O], I32, name="hid_words", align_bytes=64)
+        hid_scales = keep.tile([P, O], U8, name="hid_scales", align_bytes=64)
+        nc.vector.quantize_mx(
+            out=hid_words[:].bitcast(E4M3), scales=hid_scales[:], in_=hid[:].rearrange("p o t -> p (o t)")
+        )
+
+        pages = []
+        for i in range(4):
+            page = keep.tile([P, E], F32, name="page%d" % i, tag="reuse%d" % i, align_bytes=64)
+            nc.vector.memset(page[:], 0.0)
+            pages.append(page)
+
+        p_rows = []
+        for h in range(N // P):
+            acc = psum.tile([P, O], F32, name="acc_p%d" % h, tag="bank%d" % h)
+            nc.tensor.matmul_mx(
+                out=acc[:],
+                lhsT=wbw[:, 2 * P * h : 2 * P * (h + 1)].bitcast(E2M1),
+                lhsT_scale=wbs[:, P * h : P * (h + 1)],
+                rhs=hid_words[:].bitcast(E4M3),
+                rhs_scale=hid_scales[:],
+                start=True,
+                stop=True,
+            )
+            p_h = keep.tile([P, O], F32, name="p%d" % h)
+            if h == 0:
+                nc.vector.tensor_copy(out=p_h[:], in_=acc[:])
+            else:
+                nc.scalar.copy(out=p_h[:], in_=acc[:])
+            p_rows.append(p_h)
+
+        for h in range(N // P):
+            page_a, page_b = pages[2 * h], pages[2 * h + 1]
+            nc.vector.tensor_copy(out=page_a[:].indirect(o6[:]), in_=p_rows[h][:])
+            nc.scalar.activation(out=page_b[:].indirect(o7[:]), in_=p_rows[h][:], func=ACT.Copy)
+            y = keep.tile([P, E], F32, name="y%d" % h)
+            nc.vector.tensor_tensor(out=y[:], in0=page_a[:], in1=page_b[:], op=ALU.add)
+            nc.sync.dma_start(out=out[P * h : P * (h + 1), :], in_=y[:])

@@ -38,7 +38,7 @@ def tile_list_leadgroupboard_ahead_one_pagetwice_kernel(
             return tile
 
         def zeroed_plane(name, width):
-            plane = keep.tile([P, width], U8, name=name, align_bytes=64)
+            plane = keep.tile([P, width], U8, name=name, tag=name, align_bytes=64)
             nc.vector.memset(plane[:].bitcast(I32), 0)
             return plane
 
@@ -70,13 +70,13 @@ def tile_list_leadgroupboard_ahead_one_pagetwice_kernel(
         o2 = load_list("o2", offs2)
         xw = keep.tile([P, T], I32, name="xw", align_bytes=64)
         nc.sync.dma_start(out=xw[:], in_=xt_words[0].rearrange("p c t -> p (c t)").bitcast(I32))
-        load_plane(nc.scalar, xs, xt_scales)
+        load_plane(nc.sync, xs, xt_scales)
         w2s_stage = load_stage(nc.scalar, "w2s_stage", w2_scales)
         ww = keep.tile([P, R // 2], I32, name="ww", align_bytes=64)
         nc.sync.dma_start(out=ww[:], in_=w_words[0].bitcast(I32))
+        o3 = load_list("o3", offs3)
         w2w = keep.tile([P, R], I32, name="w2w", align_bytes=64)
         nc.sync.dma_start(out=w2w[:], in_=w2_words[0].rearrange("p c t -> p (c t)").bitcast(I32))
-        o3 = load_list("o3", offs3)
         o5 = load_list("o5", offs5)
         o4 = load_list("o4", offs4)
         wbw = keep.tile([P, 2 * N], U8, name="wbw", align_bytes=64)
@@ -106,11 +106,11 @@ def tile_list_leadgroupboard_ahead_one_pagetwice_kernel(
             nc.vector.tensor_copy(out=picked[:].bitcast(U32), in_=xw[:].bitcast(U32).indirect(offsets[:]))
             return picked
 
-        xs1 = gather_scales("xs1", o1)
-        xs2 = gather_scales("xs2", o2)
         w2s_dealt = dealt_plane("w2s_dealt", w2s_stage, w2s)
         xw1 = gather_words("xw1", o1)
+        xs1 = gather_scales("xs1", o1)
         xw2 = gather_words("xw2", o2)
+        xs2 = gather_scales("xs2", o2)
 
         ww_dealt = keep.tile([P, 2 * R], U8, name="ww_dealt", align_bytes=64)
         ww_out = ww_dealt[:].bitcast(U16).rearrange("p (t m) -> p t m", t=PACK)
@@ -183,8 +183,8 @@ def tile_list_leadgroupboard_ahead_one_pagetwice_kernel(
         )
 
         pages = []
-        for i in range(4):
-            page = keep.tile([P, E], F32, name="page%d" % i, tag="reuse%d" % i, align_bytes=64)
+        for i, tag in enumerate(("xs", "reuse0", "reuse2", "reuse3")):
+            page = keep.tile([P, E], F32, name="page%d" % i, tag=tag, align_bytes=64)
             nc.vector.memset(page[:], 0.0)
             pages.append(page)
 
@@ -211,6 +211,8 @@ def tile_list_leadgroupboard_ahead_one_pagetwice_kernel(
             page_a, page_b = pages[2 * h], pages[2 * h + 1]
             nc.vector.tensor_copy(out=page_a[:].indirect(o6[:]), in_=p_rows[h][:])
             nc.scalar.activation(out=page_b[:].indirect(o7[:]), in_=p_rows[h][:], func=ACT.Copy)
-            y = keep.tile([P, E], F32, name="y%d" % h)
-            nc.vector.tensor_tensor(out=y[:], in0=page_a[:], in1=page_b[:], op=ALU.add)
-            nc.sync.dma_start(out=out[P * h : P * (h + 1), :], in_=y[:])
+            parts = ((0, E, nc.sync),) if h == 0 else ((0, E // 2, nc.scalar), (E // 2, E, nc.sync))
+            for e0, e1, queue in parts:
+                y = keep.tile([P, e1 - e0], F32, name="y%d_%d" % (h, e0))
+                nc.vector.tensor_tensor(out=y[:], in0=page_a[:, e0:e1], in1=page_b[:, e0:e1], op=ALU.add)
+                queue.dma_start(out=out[P * h : P * (h + 1), e0:e1], in_=y[:])

@@ -68,12 +68,12 @@ def tile_list_leadgroupboard_ahead_one_pagetwice_kernel(
         o1 = load_list("o1", offs)
         ws_stage = load_stage(nc.scalar, "ws_stage", w_scales)
         o2 = load_list("o2", offs2)
-        xw = keep.tile([P, T], I32, name="xw", align_bytes=64)
+        xw = keep.tile([P, T], I32, name="xw", tag="xw", align_bytes=64)
         nc.sync.dma_start(out=xw[:], in_=xt_words[0].rearrange("p c t -> p (c t)").bitcast(I32))
-        load_plane(nc.sync, xs, xt_scales)
-        w2s_stage = load_stage(nc.scalar, "w2s_stage", w2_scales)
+        load_plane(nc.scalar, xs, xt_scales)
         ww = keep.tile([P, R // 2], I32, name="ww", align_bytes=64)
         nc.sync.dma_start(out=ww[:], in_=w_words[0].bitcast(I32))
+        w2s_stage = load_stage(nc.sync, "w2s_stage", w2_scales)
         o3 = load_list("o3", offs3)
         w2w = keep.tile([P, R], I32, name="w2w", align_bytes=64)
         nc.sync.dma_start(out=w2w[:], in_=w2_words[0].rearrange("p c t -> p (c t)").bitcast(I32))
@@ -101,31 +101,28 @@ def tile_list_leadgroupboard_ahead_one_pagetwice_kernel(
             nc.vector.tensor_copy(out=picked[:], in_=xs[:].indirect(offsets[:]))
             return picked
 
-        def gather_words(name, offsets):
-            picked = keep.tile([P, J], I32, name=name, align_bytes=64)
-            nc.vector.tensor_copy(out=picked[:].bitcast(U32), in_=xw[:].bitcast(U32).indirect(offsets[:]))
-            return picked
 
-        w2s_dealt = dealt_plane("w2s_dealt", w2s_stage, w2s)
-        xw1 = gather_words("xw1", o1)
         xs1 = gather_scales("xs1", o1)
-        xw2 = gather_words("xw2", o2)
         xs2 = gather_scales("xs2", o2)
+        picked_words = keep.tile([P, 2 * J], I32, name="picked_words", tag="xs", align_bytes=64)
+        xw1, xw2 = picked_words[:, :J], picked_words[:, J:]
+        for picked, offsets in ((xw1, o1), (xw2, o2)):
+            nc.vector.tensor_copy(out=picked.bitcast(U32), in_=xw[:].bitcast(U32).indirect(offsets[:]))
+        w2s_dealt = dealt_plane("w2s_dealt", w2s_stage, w2s)
 
         ww_dealt = keep.tile([P, 2 * R], U8, name="ww_dealt", align_bytes=64)
         ww_out = ww_dealt[:].bitcast(U16).rearrange("p (t m) -> p t m", t=PACK)
         ww_in = ww[:].bitcast(U16).rearrange("p (m t) -> p t m", t=PACK)
-        nc.scalar.copy(out=ww_out[:, 0, :], in_=ww_in[:, 0, :])
-        nc.scalar.copy(out=ww_out[:, 1:, :], in_=ww_in[:, 1:, :])
 
         a_rows = []
         for t in range(PACK):
+            nc.scalar.copy(out=ww_out[:, t, :], in_=ww_in[:, t, :])
             acc = psum.tile([P, J], F32, name="acc_a%d" % t, tag="bank%d" % t)
             nc.tensor.matmul_mx(
                 out=acc[:],
                 lhsT=ww_dealt[:, 2 * P * t : 2 * P * (t + 1)].bitcast(E2M1),
                 lhsT_scale=ws_dealt[:, P * t : P * (t + 1)],
-                rhs=xw1[:].bitcast(E5M2),
+                rhs=xw1.bitcast(E5M2),
                 rhs_scale=xs1[:],
                 start=True,
                 stop=True,
@@ -150,7 +147,7 @@ def tile_list_leadgroupboard_ahead_one_pagetwice_kernel(
                 out=acc[:],
                 lhsT=w2w_dealt[:, P * t : P * (t + 1)].bitcast(E4M3),
                 lhsT_scale=w2s_dealt[:, P * t : P * (t + 1)],
-                rhs=xw2[:].bitcast(E5M2),
+                rhs=xw2.bitcast(E5M2),
                 rhs_scale=xs2[:],
                 start=True,
                 stop=True,
@@ -183,7 +180,7 @@ def tile_list_leadgroupboard_ahead_one_pagetwice_kernel(
         )
 
         pages = []
-        for i, tag in enumerate(("xs", "reuse0", "reuse2", "reuse3")):
+        for i, tag in enumerate(("reuse0", "reuse1", "reuse2", "reuse3")):
             page = keep.tile([P, E], F32, name="page%d" % i, tag=tag, align_bytes=64)
             nc.vector.memset(page[:], 0.0)
             pages.append(page)
@@ -211,8 +208,6 @@ def tile_list_leadgroupboard_ahead_one_pagetwice_kernel(
             page_a, page_b = pages[2 * h], pages[2 * h + 1]
             nc.vector.tensor_copy(out=page_a[:].indirect(o6[:]), in_=p_rows[h][:])
             nc.scalar.activation(out=page_b[:].indirect(o7[:]), in_=p_rows[h][:], func=ACT.Copy)
-            parts = ((0, E, nc.sync),) if h == 0 else ((0, E // 2, nc.scalar), (E // 2, E, nc.sync))
-            for e0, e1, queue in parts:
-                y = keep.tile([P, e1 - e0], F32, name="y%d_%d" % (h, e0))
-                nc.vector.tensor_tensor(out=y[:], in0=page_a[:, e0:e1], in1=page_b[:, e0:e1], op=ALU.add)
-                queue.dma_start(out=out[P * h : P * (h + 1), e0:e1], in_=y[:])
+            y = keep.tile([P, E], F32, name="y%d" % h)
+            nc.vector.tensor_tensor(out=y[:], in0=page_a[:], in1=page_b[:], op=ALU.add)
+            nc.sync.dma_start(out=out[P * h : P * (h + 1), :], in_=y[:])

@@ -38,7 +38,7 @@ def tile_list_leadgroupboard_ahead_one_pagetwice_kernel(
             return tile
 
         def zeroed_plane(name, width):
-            plane = keep.tile([P, width], U8, name=name, tag=name, align_bytes=64)
+            plane = keep.tile([P, width], U8, name=name, align_bytes=64)
             nc.vector.memset(plane[:].bitcast(I32), 0)
             return plane
 
@@ -49,31 +49,17 @@ def tile_list_leadgroupboard_ahead_one_pagetwice_kernel(
                     in_=scales[0, 4 * q : 4 * q + 4, :].bitcast(I32),
                 )
 
-        def load_stage(queue, name, scales):
-            stage = keep.tile([4, QUADS, R // 4], I32, name=name)
-            queue.dma_start(out=stage[:], in_=scales[0].bitcast(I32).rearrange("(q r) c -> r q c", r=4))
-            return stage
-
-        def dealt_plane(name, stage, plane):
-            for q in range(QUADS):
-                nc.vector.tensor_copy(out=plane[32 * q : 32 * q + 4, :].bitcast(I32), in_=stage[:, q, :])
-            dealt = keep.tile([P, R], U8, name=name, align_bytes=64)
-            nc.vector.tensor_copy(
-                out=dealt[:].rearrange("p (t m) -> p t m", t=PACK),
-                in_=plane[:].rearrange("p (m t) -> p t m", t=PACK),
-            )
-            return dealt
-
         xs = zeroed_plane("xs", T)
         o1 = load_list("o1", offs)
-        ws_stage = load_stage(nc.scalar, "ws_stage", w_scales)
+        stage = keep.tile([4, 2, QUADS, R // 4], I32, name="stage")
+        for i, scales in enumerate((w_scales, w2_scales)):
+            nc.scalar.dma_start(out=stage[:, i], in_=scales[0].bitcast(I32).rearrange("(q r) c -> r q c", r=4))
         o2 = load_list("o2", offs2)
-        xw = keep.tile([P, T], I32, name="xw", tag="xw", align_bytes=64)
+        xw = keep.tile([P, T], I32, name="xw", align_bytes=64)
         nc.sync.dma_start(out=xw[:], in_=xt_words[0].rearrange("p c t -> p (c t)").bitcast(I32))
         load_plane(nc.scalar, xs, xt_scales)
         ww = keep.tile([P, R // 2], I32, name="ww", align_bytes=64)
         nc.sync.dma_start(out=ww[:], in_=w_words[0].bitcast(I32))
-        w2s_stage = load_stage(nc.sync, "w2s_stage", w2_scales)
         o3 = load_list("o3", offs3)
         w2w = keep.tile([P, R], I32, name="w2w", align_bytes=64)
         nc.sync.dma_start(out=w2w[:], in_=w2_words[0].rearrange("p c t -> p (c t)").bitcast(I32))
@@ -81,8 +67,7 @@ def tile_list_leadgroupboard_ahead_one_pagetwice_kernel(
         o4 = load_list("o4", offs4)
         wbw = keep.tile([P, 2 * N], U8, name="wbw", align_bytes=64)
         nc.sync.dma_start(out=wbw[:].bitcast(I32), in_=wb_words[0].bitcast(I32))
-        ws = zeroed_plane("ws", R)
-        w2s = zeroed_plane("w2s", R)
+        spread = zeroed_plane("spread", 2 * R)
         wbs = zeroed_plane("wbs", N)
         load_plane(nc.sync, wbs, wb_scales)
         o6 = load_list("o6", offs6)
@@ -91,24 +76,34 @@ def tile_list_leadgroupboard_ahead_one_pagetwice_kernel(
         boards = []
         for t in range(PACK):
             board = keep.tile([P, C], F32, name="board%d" % t)
-            nc.vector.memset(board[:], 0.0)
+            nc.vector.memset(board[:].bitcast(I32), 0)
             boards.append(board)
 
-        ws_dealt = dealt_plane("ws_dealt", ws_stage, ws)
+        for q in range(QUADS):
+            nc.vector.tensor_copy(
+                out=spread[32 * q : 32 * q + 4, :].bitcast(I32).rearrange("r (i c) -> r i c", i=2), in_=stage[:, :, q, :]
+            )
+        dealt = keep.tile([P, 2 * R], U8, name="dealt", align_bytes=64)
+        nc.vector.tensor_copy(
+            out=dealt[:].rearrange("p (i t m) -> p i t m", i=2, t=PACK),
+            in_=spread[:].rearrange("p (i m t) -> p i t m", i=2, t=PACK),
+        )
+        ws_dealt, w2s_dealt = dealt[:, :R], dealt[:, R:]
 
         def gather_scales(name, offsets):
             picked = keep.tile([P, J], U8, name=name, align_bytes=64)
             nc.vector.tensor_copy(out=picked[:], in_=xs[:].indirect(offsets[:]))
             return picked
 
+        def gather_words(name, offsets):
+            picked = keep.tile([P, J], I32, name=name, align_bytes=64)
+            nc.vector.tensor_copy(out=picked[:].bitcast(U32), in_=xw[:].bitcast(U32).indirect(offsets[:]))
+            return picked
 
+        xw1 = gather_words("xw1", o1)
         xs1 = gather_scales("xs1", o1)
+        xw2 = gather_words("xw2", o2)
         xs2 = gather_scales("xs2", o2)
-        picked_words = keep.tile([P, 2 * J], I32, name="picked_words", tag="xs", align_bytes=64)
-        xw1, xw2 = picked_words[:, :J], picked_words[:, J:]
-        for picked, offsets in ((xw1, o1), (xw2, o2)):
-            nc.vector.tensor_copy(out=picked.bitcast(U32), in_=xw[:].bitcast(U32).indirect(offsets[:]))
-        w2s_dealt = dealt_plane("w2s_dealt", w2s_stage, w2s)
 
         ww_dealt = keep.tile([P, 2 * R], U8, name="ww_dealt", align_bytes=64)
         ww_out = ww_dealt[:].bitcast(U16).rearrange("p (t m) -> p t m", t=PACK)
@@ -122,7 +117,7 @@ def tile_list_leadgroupboard_ahead_one_pagetwice_kernel(
                 out=acc[:],
                 lhsT=ww_dealt[:, 2 * P * t : 2 * P * (t + 1)].bitcast(E2M1),
                 lhsT_scale=ws_dealt[:, P * t : P * (t + 1)],
-                rhs=xw1.bitcast(E5M2),
+                rhs=xw1[:].bitcast(E5M2),
                 rhs_scale=xs1[:],
                 start=True,
                 stop=True,
@@ -133,21 +128,20 @@ def tile_list_leadgroupboard_ahead_one_pagetwice_kernel(
             a_rows.append(a_t)
 
         w2w_dealt = keep.tile([P, R], I32, name="w2w_dealt", align_bytes=64)
-        nc.scalar.copy(
-            out=w2w_dealt[:].bitcast(U32).rearrange("p (t m) -> p t m", t=PACK),
-            in_=w2w[:].bitcast(U32).rearrange("p (m t) -> p t m", t=PACK),
-        )
+        w2w_out = w2w_dealt[:].bitcast(U32).rearrange("p (t m) -> p t m", t=PACK)
+        w2w_in = w2w[:].bitcast(U32).rearrange("p (m t) -> p t m", t=PACK)
 
         from_board = keep.tile([P, PACK, O], F32, name="from_board", tag="reuse0", align_bytes=64)
         from_b = keep.tile([P, PACK, O], F32, name="from_b", tag="reuse1", align_bytes=64)
         b_rows = []
         for t in range(PACK):
+            nc.scalar.copy(out=w2w_out[:, t, :], in_=w2w_in[:, t, :])
             acc = psum.tile([P, J], F32, name="acc_b%d" % t, tag="bank%d" % (PACK + t))
             nc.tensor.matmul_mx(
                 out=acc[:],
                 lhsT=w2w_dealt[:, P * t : P * (t + 1)].bitcast(E4M3),
                 lhsT_scale=w2s_dealt[:, P * t : P * (t + 1)],
-                rhs=xw2.bitcast(E5M2),
+                rhs=xw2[:].bitcast(E5M2),
                 rhs_scale=xs2[:],
                 start=True,
                 stop=True,
@@ -165,11 +159,11 @@ def tile_list_leadgroupboard_ahead_one_pagetwice_kernel(
 
         diff = keep.tile([P, PACK, O], F32, name="diff", tag="reuse2", align_bytes=64)
         hid = keep.tile([P, O, PACK], BF16, name="hid", tag="reuse3", align_bytes=64)
-        for t0 in (0, 2):
-            pair = slice(t0, t0 + 2)
+        for part in (slice(0, 2), slice(2, 3), slice(3, 4)):
             nc.vector.tensor_tensor(
-                out=diff[:, pair, :], in0=from_board[:, pair, :], in1=from_b[:, pair, :], op=ALU.subtract
+                out=diff[:, part, :], in0=from_board[:, part, :], in1=from_b[:, part, :], op=ALU.subtract
             )
+        for pair in (slice(0, 2), slice(2, 4)):
             nc.scalar.activation(
                 out=hid[:, :, pair], in_=diff[:, pair, :].rearrange("p t o -> p o t"), func=ACT.Abs
             )
@@ -180,9 +174,9 @@ def tile_list_leadgroupboard_ahead_one_pagetwice_kernel(
         )
 
         pages = []
-        for i, tag in enumerate(("reuse0", "reuse1", "reuse2", "reuse3")):
-            page = keep.tile([P, E], F32, name="page%d" % i, tag=tag, align_bytes=64)
-            nc.vector.memset(page[:], 0.0)
+        for i in range(4):
+            page = keep.tile([P, E], F32, name="page%d" % i, tag="reuse%d" % i, align_bytes=64)
+            nc.vector.memset(page[:].bitcast(I32), 0)
             pages.append(page)
 
         p_rows = []
@@ -198,10 +192,7 @@ def tile_list_leadgroupboard_ahead_one_pagetwice_kernel(
                 stop=True,
             )
             p_h = keep.tile([P, O], F32, name="p%d" % h)
-            if h == 0:
-                nc.vector.tensor_copy(out=p_h[:], in_=acc[:])
-            else:
-                nc.scalar.copy(out=p_h[:], in_=acc[:])
+            nc.scalar.copy(out=p_h[:], in_=acc[:])
             p_rows.append(p_h)
 
         for h in range(N // P):

from contextlib import ExitStack

import concourse.mybir as mybir

K, T, J, R, C, O, N, E = 512, 2048, 256, 512, 512, 128, 256, 512
FLOPS = 2 * K * R * J * 2 + 2 * R * N * O

F32 = mybir.dt.float32
BF16 = mybir.dt.bfloat16
I32 = mybir.dt.int32
U32 = mybir.dt.uint32
U16 = mybir.dt.uint16
U8 = mybir.dt.uint8
E4M3 = mybir.dt.float8_e4m3fn_x4
E5M2 = mybir.dt.float8_e5m2_x4
E2M1 = mybir.dt.float4_e2m1fn_x4
ACT = mybir.ActivationFunctionType
ALU = mybir.AluOpType

P = 128
PACK = 4
QUADS = 4


def tile_list_leadgroupboard_ahead_one_pagetwice_kernel(
    tc, xt_words, xt_scales, w_words, w_scales, w2_words, w2_scales, wb_words, wb_scales,
    offs, offs2, offs3, offs4, offs5, offs6, offs7, out,
):
    nc = tc.nc
    with ExitStack() as ctx:
        lists = ctx.enter_context(tc.tile_pool(name="lists", bufs=1))
        keep = ctx.enter_context(tc.tile_pool(name="keep", bufs=1))
        psum = ctx.enter_context(tc.psum_pool(name="psum", bufs=1))

        def load_list(name, src):
            tile = lists.tile(list(src.shape), U16, name=name)
            nc.sync.dma_start(tile[:], src)
            return tile

        def zeroed_plane(name, width):
            plane = keep.tile([P, width], U8, name=name, align_bytes=64)
            nc.vector.memset(plane[:].bitcast(I32), 0)
            return plane

        def load_plane(queue, plane, scales):
            for q in range(QUADS):
                queue.dma_start(
                    out=plane[32 * q : 32 * q + 4, :].bitcast(I32),
                    in_=scales[0, 4 * q : 4 * q + 4, :].bitcast(I32),
                )

        xs = zeroed_plane("xs", T)
        o1 = load_list("o1", offs)
        stage = keep.tile([4, 2, QUADS, R // 4], I32, name="stage")
        for i, scales in enumerate((w_scales, w2_scales)):
            nc.scalar.dma_start(out=stage[:, i], in_=scales[0].bitcast(I32).rearrange("(q r) c -> r q c", r=4))
        o2 = load_list("o2", offs2)
        xw = keep.tile([P, T], I32, name="xw", align_bytes=64)
        nc.sync.dma_start(out=xw[:], in_=xt_words[0].rearrange("p c t -> p (c t)").bitcast(I32))
        load_plane(nc.scalar, xs, xt_scales)
        ww = keep.tile([P, R // 2], I32, name="ww", align_bytes=64)
        nc.sync.dma_start(out=ww[:], in_=w_words[0].bitcast(I32))
        o3 = load_list("o3", offs3)
        w2w = keep.tile([P, R], I32, name="w2w", align_bytes=64)
        nc.sync.dma_start(out=w2w[:], in_=w2_words[0].rearrange("p c t -> p (c t)").bitcast(I32))
        o5 = load_list("o5", offs5)
        o4 = load_list("o4", offs4)
        wbw = keep.tile([P, 2 * N], U8, name="wbw", align_bytes=64)
        nc.sync.dma_start(out=wbw[:].bitcast(I32), in_=wb_words[0].bitcast(I32))
        spread = zeroed_plane("spread", 2 * R)
        wbs = zeroed_plane("wbs", N)
        load_plane(nc.sync, wbs, wb_scales)
        o6 = load_list("o6", offs6)
        o7 = load_list("o7", offs7)

        boards = []
        for t in range(PACK):
            board = keep.tile([P, C], F32, name="board%d" % t)
            nc.vector.memset(board[:].bitcast(I32), 0)
            boards.append(board)

        for q in range(QUADS):
            nc.vector.tensor_copy(
                out=spread[32 * q : 32 * q + 4, :].bitcast(I32).rearrange("r (i c) -> r i c", i=2), in_=stage[:, :, q, :]
            )
        dealt = keep.tile([P, 2 * R], U8, name="dealt", align_bytes=64)
        nc.vector.tensor_copy(
            out=dealt[:].rearrange("p (i t m) -> p i t m", i=2, t=PACK),
            in_=spread[:].rearrange("p (i m t) -> p i t m", i=2, t=PACK),
        )
        ws_dealt, w2s_dealt = dealt[:, :R], dealt[:, R:]

        def gather_scales(name, offsets):
            picked = keep.tile([P, J], U8, name=name, align_bytes=64)
            nc.vector.tensor_copy(out=picked[:], in_=xs[:].indirect(offsets[:]))
            return picked

        def gather_words(name, offsets):
            picked = keep.tile([P, J], I32, name=name, align_bytes=64)
            nc.vector.tensor_copy(out=picked[:].bitcast(U32), in_=xw[:].bitcast(U32).indirect(offsets[:]))
            return picked

        xw1 = gather_words("xw1", o1)
        xs1 = gather_scales("xs1", o1)
        xw2 = gather_words("xw2", o2)
        xs2 = gather_scales("xs2", o2)

        ww_dealt = keep.tile([P, 2 * R], U8, name="ww_dealt", align_bytes=64)
        ww_out = ww_dealt[:].bitcast(U16).rearrange("p (t m) -> p t m", t=PACK)
        ww_in = ww[:].bitcast(U16).rearrange("p (m t) -> p t m", t=PACK)

        a_rows = []
        for t in range(PACK):
            nc.scalar.copy(out=ww_out[:, t, :], in_=ww_in[:, t, :])
            acc = psum.tile([P, J], F32, name="acc_a%d" % t, tag="bank%d" % t)
            nc.tensor.matmul_mx(
                out=acc[:],
                lhsT=ww_dealt[:, 2 * P * t : 2 * P * (t + 1)].bitcast(E2M1),
                lhsT_scale=ws_dealt[:, P * t : P * (t + 1)],
                rhs=xw1[:].bitcast(E5M2),
                rhs_scale=xs1[:],
                start=True,
                stop=True,
            )
            a_t = keep.tile([P, J], F32, name="a%d" % t)
            nc.scalar.copy(out=a_t[:], in_=acc[:])
            nc.vector.tensor_copy(out=boards[t][:].indirect(o3[:]), in_=a_t[:])
            a_rows.append(a_t)

        w2w_dealt = keep.tile([P, R], I32, name="w2w_dealt", align_bytes=64)
        w2w_out = w2w_dealt[:].bitcast(U32).rearrange("p (t m) -> p t m", t=PACK)
        w2w_in = w2w[:].bitcast(U32).rearrange("p (m t) -> p t m", t=PACK)

        from_board = keep.tile([P, PACK, O], F32, name="from_board", tag="reuse0", align_bytes=64)
        from_b = keep.tile([P, PACK, O], F32, name="from_b", tag="reuse1", align_bytes=64)
        b_rows = []
        for t in range(PACK):
            nc.scalar.copy(out=w2w_out[:, t, :], in_=w2w_in[:, t, :])
            acc = psum.tile([P, J], F32, name="acc_b%d" % t, tag="bank%d" % (PACK + t))
            nc.tensor.matmul_mx(
                out=acc[:],
                lhsT=w2w_dealt[:, P * t : P * (t + 1)].bitcast(E4M3),
                lhsT_scale=w2s_dealt[:, P * t : P * (t + 1)],
                rhs=xw2[:].bitcast(E5M2),
                rhs_scale=xs2[:],
                start=True,
                stop=True,
            )
            b_t = keep.tile([P, J], F32, name="b%d" % t)
            nc.scalar.copy(out=b_t[:], in_=acc[:])
            nc.scalar.activation(
                out=from_b[:, t, :], in_=b_t[:].indirect(o5[:]), func=ACT.Copy, scale=a_rows[t][:, 0:1]
            )
            b_rows.append(b_t)
        for t in range(PACK):
            nc.scalar.activation(
                out=from_board[:, t, :], in_=boards[t][:].indirect(o4[:]), func=ACT.Copy, scale=b_rows[t][:, 0:1]
            )

        diff = keep.tile([P, PACK, O], F32, name="diff", tag="reuse2", align_bytes=64)
        hid = keep.tile([P, O, PACK], BF16, name="hid", tag="reuse3", align_bytes=64)
        for part in (slice(0, 2), slice(2, 3), slice(3, 4)):
            nc.vector.tensor_tensor(
                out=diff[:, part, :], in0=from_board[:, part, :], in1=from_b[:, part, :], op=ALU.subtract
            )
        for pair in (slice(0, 2), slice(2, 4)):
            nc.scalar.activation(
                out=hid[:, :, pair], in_=diff[:, pair, :].rearrange("p t o -> p o t"), func=ACT.Abs
            )
        hid_words = keep.tile([P, O], I32, name="hid_words", align_bytes=64)
        hid_scales = keep.tile([P, O], U8, name="hid_scales", align_bytes=64)
        nc.vector.quantize_mx(
            out=hid_words[:].bitcast(E4M3), scales=hid_scales[:], in_=hid[:].rearrange("p o t -> p (o t)")
        )

        pages = []
        for i in range(4):
            page = keep.tile([P, E], F32, name="page%d" % i, tag="reuse%d" % i, align_bytes=64)
            nc.vector.memset(page[:].bitcast(I32), 0)
            pages.append(page)

        p_rows = []
        for h in range(N // P):
            acc = psum.tile([P, O], F32, name="acc_p%d" % h, tag="bank%d" % h)
            nc.tensor.matmul_mx(
                out=acc[:],
                lhsT=wbw[:, 2 * P * h : 2 * P * (h + 1)].bitcast(E2M1),
                lhsT_scale=wbs[:, P * h : P * (h + 1)],
                rhs=hid_words[:].bitcast(E4M3),
                rhs_scale=hid_scales[:],
                start=True,
                stop=True,
            )
            p_h = keep.tile([P, O], F32, name="p%d" % h)
            nc.scalar.copy(out=p_h[:], in_=acc[:])
            p_rows.append(p_h)

        for h in range(N // P):
            page_a, page_b = pages[2 * h], pages[2 * h + 1]
            nc.vector.tensor_copy(out=page_a[:].indirect(o6[:]), in_=p_rows[h][:])
            nc.scalar.activation(out=page_b[:].indirect(o7[:]), in_=p_rows[h][:], func=ACT.Copy)
            y = keep.tile([P, E], F32, name="y%d" % h)
            nc.vector.tensor_tensor(out=y[:], in0=page_a[:], in1=page_b[:], op=ALU.add)
            nc.sync.dma_start(out=out[P * h : P * (h + 1), :], in_=y[:])
